import numpy as np
import ml_dtypes


def mxq(x, axis, fmt="e4m3"):
    dtype, down = {"e4m3": (ml_dtypes.float8_e4m3fn, 7), "e5m2": (ml_dtypes.float8_e5m2, 14)}[fmt]
    v = np.moveaxis(np.asarray(x, np.float32).astype(ml_dtypes.bfloat16).astype(np.float64), axis, -1)
    blocks = v.reshape(v.shape[:-1] + (-1, 32))
    amax = np.abs(blocks).max(-1, keepdims=True)
    byte = np.maximum(np.where(amax > 0, np.frexp(amax)[1] - 1 + 127, 0) - down, 1)
    scale = np.exp2(byte - 127.0)
    codes = (blocks / scale).astype(np.float32).astype(dtype).astype(np.float64)
    return np.moveaxis((codes * scale).reshape(v.shape), -1, axis)


WIDE = False


def mx_kscale(k):
    if not WIDE:
        return np.ones(k)
    levels = np.array([10, -10, 5, -5, 0])
    if k % 512:
        return np.exp2(np.random.permutation(np.resize(levels, k // 32))).repeat(32)
    a = np.empty((k // 512, 16))
    for p in range(k // 512):
        a[p, :8] = np.random.permutation(np.resize(levels, 8))
        for g in range(8):
            far = levels[np.abs(levels - a[p, g]) >= 10]
            a[p, g + 8] = far[np.random.randint(len(far))]
    return np.exp2(a.ravel()).repeat(32)


def f64(x):
    return np.asarray(x).astype(np.float64)


def striped(idx):
    return np.tile(idx.reshape(-1, 16).T, (8, 1)).astype(np.uint16)


def unstriped(offs):
    return offs[:16].T.reshape(-1).astype(np.int64)


def pack_weight(w):
    k, n = w.shape
    w = f64(np.asarray(w, np.float32).astype(ml_dtypes.bfloat16)).reshape(k // 32, 32, n)
    amax = np.abs(w).max(1)
    byte = np.clip(np.where(amax > 0, np.frexp(amax)[1] - 1 + 127 - 7, 1), 1, 254)
    scaled = (w * np.exp2(127.0 - byte)[:, None, :]).reshape(k, n).astype(np.float32)
    words = np.ascontiguousarray(scaled.reshape(k // 512, 128, 4, n).transpose(0, 1, 3, 2)).astype(ml_dtypes.float8_e4m3fn).view(np.uint8)
    return words, np.ascontiguousarray(byte.astype(np.uint8).reshape(k // 512, 16, n))


def unpack_weight(words, scales):
    g, p, n, _ = words.shape
    vals = np.ascontiguousarray(words).view(ml_dtypes.float8_e4m3fn).astype(np.float64) * np.repeat(np.exp2(scales.astype(np.float64) - 127.0), 8, axis=1)[..., None]
    return vals.transpose(0, 1, 3, 2).reshape(g * 512, n)


def relu(v):
    return np.maximum(v, 0.0)


K, T, E, C, N = 2048, 1024, 8, 128, 128


def by_expert(wq, xq):
    return np.concatenate([wq[e].T @ xq[:, e * C:(e + 1) * C] for e in range(E)], axis=1)


def setup_inputs():
    n = np.random.standard_normal
    s = mx_kscale(K)[:, None]
    packed = [pack_weight(m) for m in n((E, K, N)) / np.sqrt(K) / s[None]]
    return {
        "xT": (n((K, T)) * s).astype(np.float32),
        "w_words": np.stack([m[0] for m in packed]),
        "w_scales": np.stack([m[1] for m in packed]),
        "b": (0.3 * n((N, E))).astype(np.float32),
        "gate": np.tile(np.random.uniform(0.2, 1.0, E * C), (N, 1)).astype(np.float32),
        "offs": striped(np.random.permutation(T)[:E * C]),
    }


def reference(xT, w_words, w_scales, b, gate, offs):
    idx = unstriped(offs)
    xq = mxq(f64(xT)[:, idx], 0, "e4m3")
    w = np.stack([unpack_weight(w_words[e], w_scales[e]) for e in range(E)])
    y = by_expert(w, xq)
    y = relu(y + np.repeat(f64(b), C, axis=1))
    out = np.zeros((N, T))
    out[:, idx] = f64(gate) * y
    return out

@@ -1,0 +1,214 @@
+from contextlib import ExitStack
+
+import concourse.mybir as mybir
+
+K, T, E, C, N = 2048, 1024, 8, 128, 128
+
+F32 = mybir.dt.float32
+BF16 = mybir.dt.bfloat16
+U32 = mybir.dt.uint32
+I32 = mybir.dt.int32
+U16 = mybir.dt.uint16
+U8 = mybir.dt.uint8
+FP8X4 = mybir.dt.float8_e4m3fn_x4
+RELU = mybir.ActivationFunctionType.Relu
+COPY = mybir.ActivationFunctionType.Copy
+MULT = mybir.AluOpType.mult
+ADD = mybir.AluOpType.add
+
+P = 128
+PASSES = K // 512
+SLOTS = E * C
+HALF = SLOTS // 2
+FLOPS = 2 * K * N * SLOTS
+
+XP = 0
+VUNITS = [(1, 0), (1, 1), (2, 0), (2, 1), (3, 0), (3, 1)]
+NV = len(VUNITS)
+
+
+def tile_routed_moe_kernel(tc, xT, w_words, w_scales, b, gate, offs, out):
+    nc = tc.nc
+    with ExitStack() as ctx:
+        lists = ctx.enter_context(tc.tile_pool(name="lists", bufs=1))
+        keep = ctx.enter_context(tc.tile_pool(name="keep", bufs=1))
+        psum = ctx.enter_context(tc.psum_pool(name="psum", bufs=1))
+
+        offsets = lists.tile([P, SLOTS // 16], U16, name="offsets")
+        nc.sync.dma_start(offsets[:], offs)
+
+        raw = dict(((g, u), keep.tile([P, 2, T], F32, name="raw%d%d" % (g, u))) for g in range(PASSES) for u in range(2))
+        pairs = keep.tile([P, NV * T * 2], BF16, name="pairs")
+        pair_words = pairs[:].bitcast(U32)
+        planes = keep.tile([P, 4 * T], BF16, name="planes")
+        qin = [keep.tile([P, SLOTS * 4], BF16, name="qin%d" % g, align_bytes=64) for g in range(PASSES)]
+        gw = [keep.tile([P, 2, SLOTS], I32, name="gw%d" % g) for g in range(PASSES)]
+        codes = [keep.tile([P, SLOTS], U32, name="codes%d" % g, align_bytes=64) for g in range(PASSES)]
+        xsc = [keep.tile([P, SLOTS], U8, name="xsc%d" % g, align_bytes=64) for g in range(PASSES)]
+        w_sb = keep.tile([P, E, PASSES, N], I32, name="w_sb", align_bytes=64)
+        ws = keep.tile([P, E * PASSES, N], U8, name="ws", align_bytes=64)
+        b_sb = keep.tile([P, E], F32, name="b_sb")
+        gate_sb = keep.tile([P, SLOTS], F32, name="gate_sb")
+        y = keep.tile([P, SLOTS], F32, name="y")
+        win = keep.tile([P, T], F32, name="win")
+        acc = [psum.tile([P, C], F32, name="acc%d" % e) for e in range(E)]
+
+        nc.vector.memset(ws[:].bitcast(I32), 0)
+
+        xv = xT.rearrange("(g p t) n -> g p t n", p=P, t=4)
+
+        def load(g, u, pieces):
+            step = T // pieces
+            for c0 in range(0, T, step):
+                nc.sync.dma_start(raw[(g, u)][:, :, c0 : c0 + step], xv[g, :, 2 * u : 2 * u + 2, c0 : c0 + step])
+
+        def load_planes(u):
+            for e in range(2):
+                nc.sync.dma_start(raw[(XP, u)][:, e, :], xv[XP, :, 2 * u + e, :])
+
+        load(1, 0, 2)
+        load(1, 1, 2)
+        load(2, 0, 2)
+        load(2, 1, 2)
+        load_planes(0)
+        load(3, 0, 2)
+        load(3, 1, 2)
+        load_planes(1)
+        nc.sync.dma_start(b_sb[:], b)
+        ws_words = ws[:].bitcast(I32)
+        for q in range(4):
+            nc.sync.dma_start(
+                ws_words[32 * q : 32 * q + 4, :, :],
+                w_scales[:, :, 4 * q : 4 * q + 4, :].rearrange("e a r n -> r (e a) n").bitcast(I32),
+            )
+        for e in range(E):
+            nc.sync.dma_start(w_sb[:, e, :, :], w_words[e].rearrange("a p n r -> p a (n r)").bitcast(I32))
+            if e % 4 == 3:
+                h = e // 4
+                nc.sync.dma_start(gate_sb[:, h * HALF : (h + 1) * HALF], gate[:, h * HALF : (h + 1) * HALF])
+
+        def convert(who, dst, src):
+            if who == "v":
+                nc.vector.tensor_copy(out=dst, in_=src)
+            elif who == "s":
+                nc.scalar.copy(out=dst, in_=src)
+            else:
+                nc.gpsimd.tensor_scalar(out=dst, in0=src, scalar1=1.0, scalar2=0.0, op0=MULT, op1=ADD)
+
+        def cast(who, g, u, c0, c1):
+            r = NV - 1 - VUNITS.index((g, u))
+            dst = pairs[:, (r * T + c0) * 2 : (r * T + c1) * 2].rearrange("p (n e) -> p n e", e=2)
+            src = raw[(g, u)][:, :, c0:c1].rearrange("p e n -> p n e")
+            convert(who, dst, src)
+
+        def cast_plane(who, t):
+            dst = planes[:, t * T : (t + 1) * T]
+            src = raw[(XP, t // 2)][:, t % 2, :]
+            convert(who, dst, src)
+
+        def gather_plane(t, j0, j1):
+            dst = qin[XP][:].rearrange("p (j t) -> p j t", t=4)[:, j0:j1, t]
+            nc.scalar.activation(
+                out=dst, in_=planes[:, t * T : (t + 1) * T].indirect(offsets[:, j0 // 16 : j1 // 16]), func=COPY
+            )
+
+        def gather(g, u, j0, j1):
+            r = NV - 1 - VUNITS.index((g, u))
+            width = 2 * T if r < NV - 1 else T
+            window = pair_words[:, r * T : r * T + width]
+            nc.vector.tensor_copy(out=gw[g][:, u, j0:j1].bitcast(U32), in_=window.indirect(offsets[:, j0 // 16 : j1 // 16]))
+
+        def interleave(g, j0, j1):
+            dst = qin[g][:, 4 * j0 : 4 * j1].bitcast(I32).rearrange("p (j u) -> p j u", u=2)
+            nc.vector.tensor_copy(out=dst, in_=gw[g][:, :, j0:j1].rearrange("p u j -> p j u"))
+
+        def quantise(g, j0, j1):
+            nc.vector.quantize_mx(
+                out=codes[g][:, j0:j1].bitcast(FP8X4),
+                scales=xsc[g][:, j0:j1],
+                in_=qin[g][:, 4 * j0 : 4 * j1],
+            )
+
+        def multiply(g, e, start, stop):
+            cols = slice(e * C, (e + 1) * C)
+            nc.tensor.matmul_mx(
+                out=acc[e][:],
+                lhsT=w_sb[:, e, g, :].bitcast(FP8X4),
+                lhsT_scale=ws[:, e * PASSES + g, :],
+                rhs=codes[g][:, cols].bitcast(FP8X4),
+                rhs_scale=xsc[g][:, cols],
+                start=start,
+                stop=stop,
+            )
+
+        def finish(e):
+            cols = slice(e * C, (e + 1) * C)
+            nc.scalar.activation(out=y[:, cols], in_=acc[e][:], func=RELU, bias=b_sb[:, e : e + 1])
+
+        def scatter(j0, j1):
+            nc.vector.tensor_tensor(
+                out=win[:].indirect(offsets[:, j0 // 16 : j1 // 16]), in0=y[:, j0:j1], in1=gate_sb[:, j0:j1], op=MULT
+            )
+
+        FIRST = range(E // 2)
+        SECOND = range(E // 2, E)
+        cast("v", 1, 0, 0, HALF)
+        cast("v", 1, 0, HALF, T)
+        cast("s", 1, 1, 0, HALF)
+        cast("s", 1, 1, HALF, T)
+        cast("s", 2, 0, 0, HALF)
+        cast("s", 2, 0, HALF, T)
+        cast("s", 2, 1, 0, HALF)
+        cast("s", 2, 1, HALF, T)
+        cast_plane("g", 0)
+        cast_plane("g", 1)
+        cast("g", 3, 0, 0, HALF)
+        cast("g", 3, 0, HALF, T)
+        cast("g", 3, 1, 0, HALF)
+        cast("g", 3, 1, HALF, T)
+        cast_plane("g", 2)
+        cast_plane("g", 3)
+        gather(1, 0, 0, HALF)
+        gather(1, 0, HALF, SLOTS)
+        gather(1, 1, 0, SLOTS)
+        gather(2, 0, 0, SLOTS)
+        interleave(1, 0, SLOTS)
+        gather(2, 1, 0, SLOTS)
+        quantise(1, 0, SLOTS)
+        gather_plane(0, 0, HALF)
+        gather_plane(1, 0, HALF)
+        gather_plane(0, HALF, SLOTS)
+        gather_plane(1, HALF, SLOTS)
+        gather(3, 0, 0, HALF)
+        interleave(2, 0, SLOTS)
+        gather(3, 1, 0, HALF)
+        quantise(2, 0, SLOTS)
+        for e in range(E):
+            multiply(1, e, True, False)
+            multiply(2, e, False, False)
+        gather_plane(2, 0, HALF)
+        gather_plane(3, 0, HALF)
+        gather_plane(2, HALF, SLOTS)
+        gather_plane(3, HALF, SLOTS)
+        interleave(3, 0, HALF)
+        gather(3, 0, HALF, SLOTS)
+        quantise(XP, 0, HALF)
+        for e in FIRST:
+            multiply(XP, e, False, False)
+        quantise(3, 0, HALF)
+        for e in FIRST:
+            multiply(3, e, False, True)
+            finish(e)
+        gather(3, 1, HALF, SLOTS)
+        quantise(XP, HALF, SLOTS)
+        for e in SECOND:
+            multiply(XP, e, False, False)
+        interleave(3, HALF, SLOTS)
+        quantise(3, HALF, SLOTS)
+        for e in SECOND:
+            multiply(3, e, False, True)
+            finish(e)
+        scatter(0, HALF)
+        scatter(HALF, SLOTS)
+
+        nc.sync.dma_start(out, win[:])

@@ -62,18 +62,19 @@ def tile_routed_moe_kernel(tc, xT, w_words, w_scales, b, gate, offs, out):
             for c0 in range(0, T, step):
                 nc.sync.dma_start(raw[(g, u)][:, :, c0 : c0 + step], xv[g, :, 2 * u : 2 * u + 2, c0 : c0 + step])
 
-        def load_planes(u):
-            for e in range(2):
-                nc.sync.dma_start(raw[(XP, u)][:, e, :], xv[XP, :, 2 * u + e, :])
+        def load_plane(t):
+            nc.sync.dma_start(raw[(XP, t // 2)][:, t % 2, :], xv[XP, :, t, :])
 
         load(1, 0, 2)
         load(1, 1, 2)
         load(2, 0, 2)
         load(2, 1, 2)
-        load_planes(0)
+        load_plane(0)
+        load_plane(1)
         load(3, 0, 2)
+        load_plane(2)
         load(3, 1, 2)
-        load_planes(1)
+        load_plane(3)
         nc.sync.dma_start(b_sb[:], b)
         ws_words = ws[:].bitcast(I32)
         for q in range(4):
@@ -164,9 +165,9 @@ def tile_routed_moe_kernel(tc, xT, w_words, w_scales, b, gate, offs, out):
         cast_plane("g", 1)
         cast("g", 3, 0, 0, HALF)
         cast("g", 3, 0, HALF, T)
+        cast_plane("g", 2)
         cast("g", 3, 1, 0, HALF)
         cast("g", 3, 1, HALF, T)
-        cast_plane("g", 2)
         cast_plane("g", 3)
         gather(1, 0, 0, HALF)
         gather(1, 0, HALF, SLOTS)

@@ -70,8 +70,8 @@ def tile_routed_moe_kernel(tc, xT, w_words, w_scales, b, gate, offs, out):
         load(2, 0, 2)
         load(2, 1, 2)
         load_plane(0)
-        load_plane(1)
         load(3, 0, 2)
+        load_plane(1)
         load_plane(2)
         load(3, 1, 2)
         load_plane(3)
@@ -162,9 +162,9 @@ def tile_routed_moe_kernel(tc, xT, w_words, w_scales, b, gate, offs, out):
         cast("s", 2, 1, 0, HALF)
         cast("s", 2, 1, HALF, T)
         cast_plane("g", 0)
-        cast_plane("g", 1)
         cast("g", 3, 0, 0, HALF)
         cast("g", 3, 0, HALF, T)
+        cast_plane("g", 1)
         cast_plane("g", 2)
         cast("g", 3, 1, 0, HALF)
         cast("g", 3, 1, HALF, T)

@@ -103,15 +103,15 @@ def tile_routed_moe_kernel(tc, xT, w_words, w_scales, b, gate, offs, out):
             convert(who, dst, src)
 
         def cast_plane(who, t):
-            dst = planes[:, t * T : (t + 1) * T]
+            dst = planes[:, (3 - t) * T : (4 - t) * T]
             src = raw[(XP, t // 2)][:, t % 2, :]
             convert(who, dst, src)
 
         def gather_plane(t, j0, j1):
             dst = qin[XP][:].rearrange("p (j t) -> p j t", t=4)[:, j0:j1, t]
-            nc.scalar.activation(
-                out=dst, in_=planes[:, t * T : (t + 1) * T].indirect(offsets[:, j0 // 16 : j1 // 16]), func=COPY
-            )
+            width = T if j1 - j0 < SLOTS else 2 * T
+            window = planes[:, (3 - t) * T : (3 - t) * T + width]
+            nc.scalar.activation(out=dst, in_=window.indirect(offsets[:, j0 // 16 : j1 // 16]), func=COPY)
 
         def gather(g, u, j0, j1):
             r = NV - 1 - VUNITS.index((g, u))
@@ -177,9 +177,9 @@ def tile_routed_moe_kernel(tc, xT, w_words, w_scales, b, gate, offs, out):
         gather(2, 1, 0, SLOTS)
         quantise(1, 0, SLOTS)
         gather_plane(0, 0, HALF)
-        gather_plane(1, 0, HALF)
         gather_plane(0, HALF, SLOTS)
-        gather_plane(1, HALF, SLOTS)
+        gather_plane(1, 0, SLOTS)
+        gather_plane(2, 0, SLOTS)
         gather(3, 0, 0, HALF)
         interleave(2, 0, SLOTS)
         gather(3, 1, 0, HALF)
@@ -187,9 +187,7 @@ def tile_routed_moe_kernel(tc, xT, w_words, w_scales, b, gate, offs, out):
         for e in range(E):
             multiply(1, e, True, False)
             multiply(2, e, False, False)
-        gather_plane(2, 0, HALF)
         gather_plane(3, 0, HALF)
-        gather_plane(2, HALF, SLOTS)
         gather_plane(3, HALF, SLOTS)
         interleave(3, 0, HALF)
         gather(3, 0, HALF, SLOTS)
@@ -209,7 +207,7 @@ def tile_routed_moe_kernel(tc, xT, w_words, w_scales, b, gate, offs, out):
         for e in SECOND:
             multiply(3, e, False, True)
             finish(e)
-        scatter(0, HALF)
-        scatter(HALF, SLOTS)
+        for j0 in range(0, SLOTS, 2 * C):
+            scatter(j0, j0 + 2 * C)
 
         nc.sync.dma_start(out, win[:])

@@ -180,17 +180,16 @@ def tile_routed_moe_kernel(tc, xT, w_words, w_scales, b, gate, offs, out):
         gather_plane(0, HALF, SLOTS)
         gather_plane(1, 0, SLOTS)
         gather_plane(2, 0, SLOTS)
-        gather(3, 0, 0, HALF)
+        gather(3, 0, 0, SLOTS)
         interleave(2, 0, SLOTS)
-        gather(3, 1, 0, HALF)
+        gather(3, 1, 0, SLOTS)
         quantise(2, 0, SLOTS)
         for e in range(E):
             multiply(1, e, True, False)
             multiply(2, e, False, False)
         gather_plane(3, 0, HALF)
         gather_plane(3, HALF, SLOTS)
-        interleave(3, 0, HALF)
-        gather(3, 0, HALF, SLOTS)
+        interleave(3, 0, SLOTS)
         quantise(XP, 0, HALF)
         for e in FIRST:
             multiply(XP, e, False, False)
@@ -198,11 +197,9 @@ def tile_routed_moe_kernel(tc, xT, w_words, w_scales, b, gate, offs, out):
         for e in FIRST:
             multiply(3, e, False, True)
             finish(e)
-        gather(3, 1, HALF, SLOTS)
         quantise(XP, HALF, SLOTS)
         for e in SECOND:
             multiply(XP, e, False, False)
-        interleave(3, HALF, SLOTS)
         quantise(3, HALF, SLOTS)
         for e in SECOND:
             multiply(3, e, False, True)

@@ -37,7 +37,8 @@ def tile_routed_moe_kernel(tc, xT, w_words, w_scales, b, gate, offs, out):
         offsets = lists.tile([P, SLOTS // 16], U16, name="offsets")
         nc.sync.dma_start(offsets[:], offs)
 
-        raw = dict(((g, u), keep.tile([P, 2, T], F32, name="raw%d%d" % (g, u))) for g in range(PASSES) for u in range(2))
+        raw = dict((k, keep.tile([P, 2, T], F32, name="raw%d%d" % k)) for k in VUNITS)
+        raw_xp = keep.tile([P, 4, T], F32, name="raw_xp")
         pairs = keep.tile([P, NV * T * 2], BF16, name="pairs")
         pair_words = pairs[:].bitcast(U32)
         planes = keep.tile([P, 4 * T], BF16, name="planes")
@@ -62,19 +63,18 @@ def tile_routed_moe_kernel(tc, xT, w_words, w_scales, b, gate, offs, out):
             for c0 in range(0, T, step):
                 nc.sync.dma_start(raw[(g, u)][:, :, c0 : c0 + step], xv[g, :, 2 * u : 2 * u + 2, c0 : c0 + step])
 
-        def load_plane(t):
-            nc.sync.dma_start(raw[(XP, t // 2)][:, t % 2, :], xv[XP, :, t, :])
+        def load_planes(t0, t1):
+            nc.sync.dma_start(raw_xp[:, t0:t1, :], xv[XP, :, t0:t1, :])
 
         load(1, 0, 2)
         load(1, 1, 2)
         load(2, 0, 2)
-        load(2, 1, 2)
-        load_plane(0)
+        load(2, 1, 1)
+        load_planes(0, 1)
         load(3, 0, 2)
-        load_plane(1)
-        load_plane(2)
-        load(3, 1, 2)
-        load_plane(3)
+        load_planes(1, 3)
+        load(3, 1, 1)
+        load_planes(3, 4)
         nc.sync.dma_start(b_sb[:], b)
         ws_words = ws[:].bitcast(I32)
         for q in range(4):
@@ -104,7 +104,7 @@ def tile_routed_moe_kernel(tc, xT, w_words, w_scales, b, gate, offs, out):
 
         def cast_plane(who, t):
             dst = planes[:, (3 - t) * T : (4 - t) * T]
-            src = raw[(XP, t // 2)][:, t % 2, :]
+            src = raw_xp[:, t, :]
             convert(who, dst, src)
 
         def gather_plane(t, j0, j1):
@@ -159,8 +159,7 @@ def tile_routed_moe_kernel(tc, xT, w_words, w_scales, b, gate, offs, out):
         cast("s", 1, 1, HALF, T)
         cast("s", 2, 0, 0, HALF)
         cast("s", 2, 0, HALF, T)
-        cast("s", 2, 1, 0, HALF)
-        cast("s", 2, 1, HALF, T)
+        cast("s", 2, 1, 0, T)
         cast_plane("g", 0)
         cast("g", 3, 0, 0, HALF)
         cast("g", 3, 0, HALF, T)
@@ -204,7 +203,8 @@ def tile_routed_moe_kernel(tc, xT, w_words, w_scales, b, gate, offs, out):
         for e in SECOND:
             multiply(3, e, False, True)
             finish(e)
-        for j0 in range(0, SLOTS, 2 * C):
-            scatter(j0, j0 + 2 * C)
+        scatter(0, HALF // 2)
+        scatter(HALF // 2, SLOTS - HALF // 2)
+        scatter(SLOTS - HALF // 2, SLOTS)
 
         nc.sync.dma_start(out, win[:])

@@ -39,9 +39,9 @@ def tile_routed_moe_kernel(tc, xT, w_words, w_scales, b, gate, offs, out):
 
         raw = dict((k, keep.tile([P, 2, T], F32, name="raw%d%d" % k)) for k in VUNITS)
         raw_xp = keep.tile([P, 4, T], F32, name="raw_xp")
-        pairs = keep.tile([P, NV * T * 2], BF16, name="pairs")
+        pairs = keep.tile([P, (NV + 1) * T * 2], BF16, name="pairs")
         pair_words = pairs[:].bitcast(U32)
-        planes = keep.tile([P, 4 * T], BF16, name="planes")
+        planes = keep.tile([P, 5 * T], BF16, name="planes")
         qin = [keep.tile([P, SLOTS * 4], BF16, name="qin%d" % g, align_bytes=64) for g in range(PASSES)]
         gw = [keep.tile([P, 2, SLOTS], I32, name="gw%d" % g) for g in range(PASSES)]
         codes = [keep.tile([P, SLOTS], U32, name="codes%d" % g, align_bytes=64) for g in range(PASSES)]
@@ -55,6 +55,8 @@ def tile_routed_moe_kernel(tc, xT, w_words, w_scales, b, gate, offs, out):
         acc = [psum.tile([P, C], F32, name="acc%d" % e) for e in range(E)]
 
         nc.vector.memset(ws[:].bitcast(I32), 0)
+        nc.gpsimd.memset(pairs[:, NV * T * 2 :].bitcast(I32), 0)
+        nc.gpsimd.memset(planes[:, 4 * T :].bitcast(I32), 0)
 
         xv = xT.rearrange("(g p t) n -> g p t n", p=P, t=4)
 
@@ -115,8 +117,7 @@ def tile_routed_moe_kernel(tc, xT, w_words, w_scales, b, gate, offs, out):
 
         def gather(g, u, j0, j1):
             r = NV - 1 - VUNITS.index((g, u))
-            width = 2 * T if r < NV - 1 else T
-            window = pair_words[:, r * T : r * T + width]
+            window = pair_words[:, r * T : r * T + 2 * T]
             nc.vector.tensor_copy(out=gw[g][:, u, j0:j1].bitcast(U32), in_=window.indirect(offsets[:, j0 // 16 : j1 // 16]))
 
         def interleave(g, j0, j1):
@@ -168,15 +169,13 @@ def tile_routed_moe_kernel(tc, xT, w_words, w_scales, b, gate, offs, out):
         cast("g", 3, 1, 0, HALF)
         cast("g", 3, 1, HALF, T)
         cast_plane("g", 3)
-        gather(1, 0, 0, HALF)
-        gather(1, 0, HALF, SLOTS)
+        gather(1, 0, 0, SLOTS)
         gather(1, 1, 0, SLOTS)
         gather(2, 0, 0, SLOTS)
         interleave(1, 0, SLOTS)
         gather(2, 1, 0, SLOTS)
         quantise(1, 0, SLOTS)
-        gather_plane(0, 0, HALF)
-        gather_plane(0, HALF, SLOTS)
+        gather_plane(0, 0, SLOTS)
         gather_plane(1, 0, SLOTS)
         gather_plane(2, 0, SLOTS)
         gather(3, 0, 0, SLOTS)
@@ -203,8 +202,8 @@ def tile_routed_moe_kernel(tc, xT, w_words, w_scales, b, gate, offs, out):
         for e in SECOND:
             multiply(3, e, False, True)
             finish(e)
-        scatter(0, HALF // 2)
-        scatter(HALF // 2, SLOTS - HALF // 2)
-        scatter(SLOTS - HALF // 2, SLOTS)
+        scatter(0, C)
+        scatter(C, HALF)
+        scatter(HALF, SLOTS)
 
         nc.sync.dma_start(out, win[:])

from contextlib import ExitStack

import concourse.mybir as mybir

K, T, E, C, N = 2048, 1024, 8, 128, 128

F32 = mybir.dt.float32
BF16 = mybir.dt.bfloat16
U32 = mybir.dt.uint32
I32 = mybir.dt.int32
U16 = mybir.dt.uint16
U8 = mybir.dt.uint8
FP8X4 = mybir.dt.float8_e4m3fn_x4
RELU = mybir.ActivationFunctionType.Relu
COPY = mybir.ActivationFunctionType.Copy
MULT = mybir.AluOpType.mult
ADD = mybir.AluOpType.add

P = 128
PASSES = K // 512
SLOTS = E * C
HALF = SLOTS // 2
FLOPS = 2 * K * N * SLOTS

XP = 0
VUNITS = [(1, 0), (1, 1), (2, 0), (2, 1), (3, 0), (3, 1)]
NV = len(VUNITS)


def tile_routed_moe_kernel(tc, xT, w_words, w_scales, b, gate, offs, out):
    nc = tc.nc
    with ExitStack() as ctx:
        lists = ctx.enter_context(tc.tile_pool(name="lists", bufs=1))
        keep = ctx.enter_context(tc.tile_pool(name="keep", bufs=1))
        psum = ctx.enter_context(tc.psum_pool(name="psum", bufs=1))

        offsets = lists.tile([P, SLOTS // 16], U16, name="offsets")
        nc.sync.dma_start(offsets[:], offs)

        raw = dict((k, keep.tile([P, 2, T], F32, name="raw%d%d" % k)) for k in VUNITS)
        raw_xp = keep.tile([P, 4, T], F32, name="raw_xp")
        pairs = keep.tile([P, (NV + 1) * T * 2], BF16, name="pairs")
        pair_words = pairs[:].bitcast(U32)
        planes = keep.tile([P, 5 * T], BF16, name="planes")
        qin = [keep.tile([P, SLOTS * 4], BF16, name="qin%d" % g, align_bytes=64) for g in range(PASSES)]
        gw = [keep.tile([P, 2, SLOTS], I32, name="gw%d" % g) for g in range(PASSES)]
        codes = [keep.tile([P, SLOTS], U32, name="codes%d" % g, align_bytes=64) for g in range(PASSES)]
        xsc = [keep.tile([P, SLOTS], U8, name="xsc%d" % g, align_bytes=64) for g in range(PASSES)]
        w_sb = keep.tile([P, E, PASSES, N], I32, name="w_sb", align_bytes=64)
        ws = keep.tile([P, E * PASSES, N], U8, name="ws", align_bytes=64)
        b_sb = keep.tile([P, E], F32, name="b_sb")
        gate_sb = keep.tile([P, SLOTS], F32, name="gate_sb")
        y = keep.tile([P, SLOTS], F32, name="y")
        win = keep.tile([P, T], F32, name="win")
        acc = [psum.tile([P, C], F32, name="acc%d" % e) for e in range(E)]

        nc.vector.memset(ws[:].bitcast(I32), 0)
        nc.gpsimd.memset(pairs[:, NV * T * 2 :].bitcast(I32), 0)
        nc.gpsimd.memset(planes[:, 4 * T :].bitcast(I32), 0)

        xv = xT.rearrange("(g p t) n -> g p t n", p=P, t=4)

        def load(g, u, pieces):
            step = T // pieces
            for c0 in range(0, T, step):
                nc.sync.dma_start(raw[(g, u)][:, :, c0 : c0 + step], xv[g, :, 2 * u : 2 * u + 2, c0 : c0 + step])

        def load_planes(t0, t1):
            nc.sync.dma_start(raw_xp[:, t0:t1, :], xv[XP, :, t0:t1, :])

        load(1, 0, 2)
        load(1, 1, 2)
        load(2, 0, 2)
        load(2, 1, 1)
        load_planes(0, 1)
        load(3, 0, 2)
        load_planes(1, 3)
        load(3, 1, 1)
        load_planes(3, 4)
        nc.sync.dma_start(b_sb[:], b)
        ws_words = ws[:].bitcast(I32)
        for q in range(4):
            nc.sync.dma_start(
                ws_words[32 * q : 32 * q + 4, :, :],
                w_scales[:, :, 4 * q : 4 * q + 4, :].rearrange("e a r n -> r (e a) n").bitcast(I32),
            )
        for e in range(E):
            nc.sync.dma_start(w_sb[:, e, :, :], w_words[e].rearrange("a p n r -> p a (n r)").bitcast(I32))
            if e % 4 == 3:
                h = e // 4
                nc.sync.dma_start(gate_sb[:, h * HALF : (h + 1) * HALF], gate[:, h * HALF : (h + 1) * HALF])

        def convert(who, dst, src):
            if who == "v":
                nc.vector.tensor_copy(out=dst, in_=src)
            elif who == "s":
                nc.scalar.copy(out=dst, in_=src)
            else:
                nc.gpsimd.tensor_scalar(out=dst, in0=src, scalar1=1.0, scalar2=0.0, op0=MULT, op1=ADD)

        def cast(who, g, u, c0, c1):
            r = NV - 1 - VUNITS.index((g, u))
            dst = pairs[:, (r * T + c0) * 2 : (r * T + c1) * 2].rearrange("p (n e) -> p n e", e=2)
            src = raw[(g, u)][:, :, c0:c1].rearrange("p e n -> p n e")
            convert(who, dst, src)

        def cast_plane(who, t):
            dst = planes[:, (3 - t) * T : (4 - t) * T]
            src = raw_xp[:, t, :]
            convert(who, dst, src)

        def gather_plane(t, j0, j1):
            dst = qin[XP][:].rearrange("p (j t) -> p j t", t=4)[:, j0:j1, t]
            width = T if j1 - j0 < SLOTS else 2 * T
            window = planes[:, (3 - t) * T : (3 - t) * T + width]
            nc.scalar.activation(out=dst, in_=window.indirect(offsets[:, j0 // 16 : j1 // 16]), func=COPY)

        def gather(g, u, j0, j1):
            r = NV - 1 - VUNITS.index((g, u))
            window = pair_words[:, r * T : r * T + 2 * T]
            nc.vector.tensor_copy(out=gw[g][:, u, j0:j1].bitcast(U32), in_=window.indirect(offsets[:, j0 // 16 : j1 // 16]))

        def interleave(g, j0, j1):
            dst = qin[g][:, 4 * j0 : 4 * j1].bitcast(I32).rearrange("p (j u) -> p j u", u=2)
            nc.vector.tensor_copy(out=dst, in_=gw[g][:, :, j0:j1].rearrange("p u j -> p j u"))

        def quantise(g, j0, j1):
            nc.vector.quantize_mx(
                out=codes[g][:, j0:j1].bitcast(FP8X4),
                scales=xsc[g][:, j0:j1],
                in_=qin[g][:, 4 * j0 : 4 * j1],
            )

        def multiply(g, e, start, stop):
            cols = slice(e * C, (e + 1) * C)
            nc.tensor.matmul_mx(
                out=acc[e][:],
                lhsT=w_sb[:, e, g, :].bitcast(FP8X4),
                lhsT_scale=ws[:, e * PASSES + g, :],
                rhs=codes[g][:, cols].bitcast(FP8X4),
                rhs_scale=xsc[g][:, cols],
                start=start,
                stop=stop,
            )

        def finish(e):
            cols = slice(e * C, (e + 1) * C)
            nc.scalar.activation(out=y[:, cols], in_=acc[e][:], func=RELU, bias=b_sb[:, e : e + 1])

        def scatter(j0, j1):
            nc.vector.tensor_tensor(
                out=win[:].indirect(offsets[:, j0 // 16 : j1 // 16]), in0=y[:, j0:j1], in1=gate_sb[:, j0:j1], op=MULT
            )

        FIRST = range(E // 2)
        SECOND = range(E // 2, E)
        cast("v", 1, 0, 0, HALF)
        cast("v", 1, 0, HALF, T)
        cast("s", 1, 1, 0, HALF)
        cast("s", 1, 1, HALF, T)
        cast("s", 2, 0, 0, HALF)
        cast("s", 2, 0, HALF, T)
        cast("s", 2, 1, 0, T)
        cast_plane("g", 0)
        cast("g", 3, 0, 0, HALF)
        cast("g", 3, 0, HALF, T)
        cast_plane("g", 1)
        cast_plane("g", 2)
        cast("g", 3, 1, 0, HALF)
        cast("g", 3, 1, HALF, T)
        cast_plane("g", 3)
        gather(1, 0, 0, SLOTS)
        gather(1, 1, 0, SLOTS)
        gather(2, 0, 0, SLOTS)
        interleave(1, 0, SLOTS)
        gather(2, 1, 0, SLOTS)
        quantise(1, 0, SLOTS)
        gather_plane(0, 0, SLOTS)
        gather_plane(1, 0, SLOTS)
        gather_plane(2, 0, SLOTS)
        gather(3, 0, 0, SLOTS)
        interleave(2, 0, SLOTS)
        gather(3, 1, 0, SLOTS)
        quantise(2, 0, SLOTS)
        for e in range(E):
            multiply(1, e, True, False)
            multiply(2, e, False, False)
        gather_plane(3, 0, HALF)
        gather_plane(3, HALF, SLOTS)
        interleave(3, 0, SLOTS)
        quantise(XP, 0, HALF)
        for e in FIRST:
            multiply(XP, e, False, False)
        quantise(3, 0, HALF)
        for e in FIRST:
            multiply(3, e, False, True)
            finish(e)
        quantise(XP, HALF, SLOTS)
        for e in SECOND:
            multiply(XP, e, False, False)
        quantise(3, HALF, SLOTS)
        for e in SECOND:
            multiply(3, e, False, True)
            finish(e)
        scatter(0, C)
        scatter(C, HALF)
        scatter(HALF, SLOTS)

        nc.sync.dma_start(out, win[:])
